import numpy as np
import ml_dtypes


def mxq(x, axis, fmt="e4m3"):
    dtype, down = {"e4m3": (ml_dtypes.float8_e4m3fn, 7), "e5m2": (ml_dtypes.float8_e5m2, 14)}[fmt]
    v = np.moveaxis(np.asarray(x, np.float32).astype(ml_dtypes.bfloat16).astype(np.float64), axis, -1)
    blocks = v.reshape(v.shape[:-1] + (-1, 32))
    amax = np.abs(blocks).max(-1, keepdims=True)
    byte = np.maximum(np.where(amax > 0, np.frexp(amax)[1] - 1 + 127, 0) - down, 1)
    scale = np.exp2(byte - 127.0)
    codes = (blocks / scale).astype(np.float32).astype(dtype).astype(np.float64)
    return np.moveaxis((codes * scale).reshape(v.shape), -1, axis)


WIDE = False


def mx_kscale(k):
    if not WIDE:
        return np.ones(k)
    levels = np.array([10, -10, 5, -5, 0])
    if k % 512:
        return np.exp2(np.random.permutation(np.resize(levels, k // 32))).repeat(32)
    a = np.empty((k // 512, 16))
    for p in range(k // 512):
        a[p, :8] = np.random.permutation(np.resize(levels, 8))
        for g in range(8):
            far = levels[np.abs(levels - a[p, g]) >= 10]
            a[p, g + 8] = far[np.random.randint(len(far))]
    return np.exp2(a.ravel()).repeat(32)


def f64(x):
    return np.asarray(x).astype(np.float64)


def striped(idx):
    return np.tile(idx.reshape(-1, 16).T, (8, 1)).astype(np.uint16)


def unstriped(offs):
    return offs[:16].T.reshape(-1).astype(np.int64)


E2M1 = np.array([0.0, 0.5, 1.0, 1.5, 2.0, 3.0, 4.0, 6.0, -0.0, -0.5, -1.0, -1.5, -2.0, -3.0, -4.0, -6.0])


def pack_weight(w, fmt):
    k, n = w.shape
    w = f64(np.asarray(w, np.float32).astype(ml_dtypes.bfloat16)).reshape(k // 32, 32, n)
    amax = np.abs(w).max(1)
    if fmt == "e4m3":
        byte = np.frexp(amax)[1] - 1 + 127 - 7
    else:
        mant, ex = np.frexp(amax / 6.0)
        byte = np.where(mant > 0.5, ex, ex - 1) + 127
    byte = np.clip(np.where(amax > 0, byte, 1), 1, 254)
    scaled = (w * np.exp2(127.0 - byte)[:, None, :]).reshape(k, n).astype(np.float32)
    by_word = np.ascontiguousarray(scaled.reshape(k // 512, 128, 4, n).transpose(0, 1, 3, 2))
    if fmt == "e4m3":
        words = by_word.astype(ml_dtypes.float8_e4m3fn).view(np.uint8)
    else:
        c = by_word.astype(ml_dtypes.float4_e2m1fn).view(np.uint8) & 0xF
        words = (c[..., 0::2] | (c[..., 1::2] << 4)).reshape(k // 512, 128, 2 * n)
    return np.ascontiguousarray(words), np.ascontiguousarray(byte.astype(np.uint8).reshape(k // 512, 16, n))


def unpack_weight(words, scales, fmt):
    g, _, n = scales.shape
    words = np.ascontiguousarray(words).reshape(g, 128, n, -1)
    if fmt == "e4m3":
        vals = words.view(ml_dtypes.float8_e4m3fn).astype(np.float64)
    else:
        nib = np.empty((g, 128, n, 4), np.uint8)
        nib[..., 0::2] = words & 0xF
        nib[..., 1::2] = words >> 4
        vals = E2M1[nib]
    vals = vals * np.repeat(np.exp2(scales.astype(np.float64) - 127.0), 8, axis=1)[..., None]
    return vals.transpose(0, 1, 3, 2).reshape(g * 512, n)


def gelu(v):
    return 0.5 * v * (1.0 + np.tanh(np.sqrt(2.0 / np.pi) * (v + 0.044715 * v**3)))


K, K2, H, N, T, S, P, T2 = 1024, 512, 1024, 512, 2048, 1024, 512, 2048

def setup_inputs():
    n = np.random.standard_normal
    s, s2, u = mx_kscale(K)[:, None], mx_kscale(K2)[:, None], mx_kscale(H)[:, None]
    tab_words, tab_scales = pack_weight(n((K, T)) * s, "e4m3")
    tab2_words, tab2_scales = pack_weight(n((K2, T)) * s2, "e4m3")
    w2_words, w2_scales = pack_weight(0.26 * n((K2, H)) / np.sqrt(K2) / s2, "e4m3")
    w3_words, w3_scales = pack_weight(2.3 * n((H, N)) / np.sqrt(H) / u, "e2m1")
    perm = np.random.permutation(T2)
    return {"tab_words": tab_words, "tab_scales": tab_scales, "offs": striped(np.random.permutation(T)[:S]),
            "tab2_words": tab2_words, "tab2_scales": tab2_scales, "offs2": striped(np.random.permutation(T)[:P]),
            "pos1": striped(np.random.permutation(S)[:P]),
            "w1": (0.48 * n((K, H)) / np.sqrt(K) / s).astype(np.float32),
            "least": np.random.uniform(-1.0, 0.5, H).astype(np.float32),
            "w2_words": w2_words, "w2_scales": w2_scales,
            "gain1": (np.exp(0.3 * n(H)) * u[:, 0]).astype(np.float32),
            "gain2": (np.exp(0.3 * n(H)) * u[:, 0]).astype(np.float32),
            "w3_words": w3_words, "w3_scales": w3_scales,
            "w4": (2.6 * n((H, N)) / np.sqrt(H) / u).astype(np.float32),
            "cover": np.exp(0.4 * n((N, P))).astype(np.float32),
            "page1": (0.6 * n((N, T2))).astype(np.float32),
            "wg1": np.exp(0.3 * n((128, S))).astype(np.float32),
            "wg2": np.exp(0.3 * n((128, P))).astype(np.float32),
            "offs3": striped(perm[:S]), "offs4": striped(perm[S:S + P])}

def reference(tab_words, tab_scales, offs, tab2_words, tab2_scales, offs2, pos1, w1, least, w2_words, w2_scales,
              gain1, gain2, w3_words, w3_scales, w4, cover, page1, wg1, wg2, offs3, offs4):
    v = unpack_weight(tab_words, tab_scales, "e4m3")[:, unstriped(offs)]
    v2 = unpack_weight(tab2_words, tab2_scales, "e4m3")[:, unstriped(offs2)]
    h1 = np.maximum(mxq(f64(w1), 0, "e4m3").T @ v, f64(least)[:, None])
    h2 = unpack_weight(w2_words, w2_scales, "e4m3").T @ v2
    z1 = np.tanh(h1) * f64(gain1)[:, None]
    z2 = np.sin(h2 + h1[:, unstriped(pos1)]) * f64(gain2)[:, None]
    y1 = unpack_weight(w3_words, w3_scales, "e2m1").T @ mxq(z1, 0, "e4m3")
    y2 = (mxq(f64(w4), 0, "e4m3").T @ mxq(z2, 0, "e4m3")) * f64(cover)
    out = f64(page1).copy()
    out[:, unstriped(offs3)] = np.tile(f64(wg1), (N // 128, 1)) * y1
    out[:, unstriped(offs4)] = np.tile(f64(wg2), (N // 128, 1)) * y2
    return out

@@ -1,0 +1,319 @@
+import math
+from contextlib import ExitStack
+
+import concourse.mybir as mybir
+
+F32 = mybir.dt.float32
+BF16 = mybir.dt.bfloat16
+I32 = mybir.dt.int32
+U32 = mybir.dt.uint32
+U16 = mybir.dt.uint16
+U8 = mybir.dt.uint8
+FP8X4 = mybir.dt.float8_e4m3fn_x4
+FP4X4 = mybir.dt.float4_e2m1fn_x4
+ALU = mybir.AluOpType
+ACT = mybir.ActivationFunctionType
+
+K, K2, H, N, T, S, PAIRS, T2 = 1024, 512, 1024, 512, 2048, 1024, 512, 2048
+FLOPS = 2 * (K * H * S + K2 * H * PAIRS + H * N * S + H * N * PAIRS)
+
+P = 128
+PACK = 4
+PASS = P * PACK
+HALF = 512
+PER_COL = 16
+TURN = 2.0 * math.pi
+
+
+def tile_list_cyber_exposure_features_kernel(
+    tc, tab_words, tab_scales, offs, tab2_words, tab2_scales, offs2, pos1, w1, least, w2_words, w2_scales,
+    gain1, gain2, w3_words, w3_scales, w4, cover, page1, wg1, wg2, offs3, offs4, out,
+):
+    nc = tc.nc
+    with ExitStack() as ctx:
+        keep = ctx.enter_context(tc.tile_pool(name="keep", bufs=1))
+        ring = ctx.enter_context(tc.tile_pool(name="ring", bufs=2))
+        psum = ctx.enter_context(tc.psum_pool(name="psum", bufs=1))
+
+        def held(shape, dtype, name):
+            return keep.tile(shape, dtype, name=name, align_bytes=64)
+
+        def load_list(src, name):
+            lst = keep.tile([P, src.shape[1]], U16, name=name)
+            nc.sync.dma_start(lst[:], src)
+            return lst
+
+        def tenant(slot, shape, dtype, name):
+            return keep.tile(shape, dtype, name=name, tag=slot, align_bytes=64)
+
+        def load_words(src, name, slot):
+            words = tenant(slot, [P, T], I32, name)
+            nc.sync.dma_start(words[:], src.rearrange("p n i -> p (n i)").bitcast(I32))
+            return words
+
+        def load_rows(src, name):
+            raw = ring.tile([P, PACK, HALF], F32, name=name, tag="raw", bufs=3)
+            nc.sync.dma_start(raw[:], src.rearrange("(p j) c -> p j c", j=PACK))
+            return raw
+
+        def load_vector(queue, src, name):
+            vec = held([P, 2, PACK], F32, name)
+            queue.dma_start(vec[:], src.rearrange("(b p t) -> p b t", p=P, t=PACK))
+            return vec
+
+        tab_plane = held([P, T], U8, "tab_plane")
+        tab2_plane = held([P, T], U8, "tab2_plane")
+        w2_plane_raw = held([P, H], U8, "w2_plane_raw")
+        w3_plane = held([P, 2, N], U8, "w3_plane")
+        nc.gpsimd.memset(tab_plane[:].bitcast(I32), 0)
+        nc.vector.memset(tab2_plane[:].bitcast(I32), 0)
+        nc.vector.memset(w2_plane_raw[:].bitcast(I32), 0)
+        nc.vector.memset(w3_plane[:].rearrange("p a n -> p (a n)").bitcast(I32), 0)
+
+        idx = load_list(offs, "idx")
+        tab_w = [load_words(tab_words[0], "tab_w0", "slot_a")]
+        for q in range(4):
+            nc.sync.dma_start(tab_plane[32 * q : 32 * q + 8, :].bitcast(I32), tab_scales[:, 4 * q : 4 * q + 4, :].bitcast(I32))
+        least_sb = load_vector(nc.sync, least, "least_sb")
+        w1_raw = {}
+        w1_raw[0, 0] = load_rows(w1[0:PASS, 0:PASS], "w1_raw00")
+        tab_w.append(load_words(tab_words[1], "tab_w1", "slot_b"))
+        idx2 = load_list(offs2, "idx2")
+        w1_raw[1, 0] = load_rows(w1[PASS:, 0:PASS], "w1_raw10")
+        pos = load_list(pos1, "pos")
+        tab2_w = load_words(tab2_words[0], "tab2_w", "slot_c")
+        w2_raw = held([P, H], I32, "w2_raw")
+        nc.sync.dma_start(w2_raw[:], w2_words[0].rearrange("p n i -> p (n i)").bitcast(I32))
+        w1_raw[0, 1] = load_rows(w1[0:PASS, PASS:], "w1_raw01")
+        w1_raw[1, 1] = load_rows(w1[PASS:, PASS:], "w1_raw11")
+        w3_w = held([P, 2, 2 * N], U8, "w3_w")
+        nc.sync.dma_start(w3_w[:].bitcast(I32), w3_words.rearrange("a p n -> p a n").bitcast(I32))
+        idx3 = load_list(offs3, "idx3")
+        idx4 = load_list(offs4, "idx4")
+        wg1_sb = held([P, S], F32, "wg1_sb")
+        nc.sync.dma_start(wg1_sb[:], wg1)
+        pages = []
+        for q in range(N // P):
+            page = held([P, T2], F32, "page%d" % q)
+            nc.sync.dma_start(page[:], page1[P * q : P * (q + 1), :])
+            pages.append(page)
+        w4_raw = [load_rows(w4[PASS * b : PASS * (b + 1), :], "w4_raw%d" % b) for b in range(2)]
+        cover_sb = ring.tile([P, N // P, PAIRS], F32, name="cover_sb", tag="raw", bufs=3)
+        nc.sync.dma_start(cover_sb[:], cover.rearrange("(q p) j -> p q j", p=P))
+        wg2_sb = held([P, PAIRS], F32, "wg2_sb")
+        nc.sync.dma_start(wg2_sb[:], wg2)
+
+        for q in range(4):
+            nc.gpsimd.dma_start(tab2_plane[32 * q : 32 * q + 4, :].bitcast(I32), tab2_scales[0, 4 * q : 4 * q + 4, :].bitcast(I32))
+        for q in range(4):
+            nc.gpsimd.dma_start(w2_plane_raw[32 * q : 32 * q + 4, :].bitcast(I32), w2_scales[0, 4 * q : 4 * q + 4, :].bitcast(I32))
+        gain1_sb = load_vector(nc.gpsimd, gain1, "gain1_sb")
+        for q in range(4):
+            nc.gpsimd.dma_start(
+                w3_plane[32 * q : 32 * q + 4, :, :].bitcast(I32),
+                w3_scales[:, 4 * q : 4 * q + 4, :].rearrange("a r n -> r a n").bitcast(I32),
+            )
+        gain2_sb = load_vector(nc.gpsimd, gain2, "gain2_sb")
+
+        def quantise(grouped, name):
+            width = grouped.shape[1] // PACK
+            codes = held([P, width], U32, name + "_codes")
+            plane = held([P, width], U8, name + "_plane")
+            nc.vector.quantize_mx(out=codes[:].bitcast(FP8X4), scales=plane[:], in_=grouped[:])
+            return codes, plane
+
+        def grouped_tile(name, width):
+            return ring.tile([P, PACK * width], BF16, name=name, tag="grouped", bufs=3, align_bytes=64)
+
+        def round_w1(a, b, vector_share, grouped):
+            dst = grouped[:].rearrange("p (t m j) -> p m j t", t=PACK, j=PACK)
+            src = w1_raw[a, b][:].rearrange("p j (m t) -> p m j t", t=PACK)
+            cut = P - vector_share
+            nc.scalar.copy(dst[:, :cut], src[:, :cut])
+            if vector_share:
+                nc.vector.tensor_copy(dst[:, cut:], src[:, cut:])
+            return grouped
+
+        def interleave(rows, name):
+            grouped = grouped_tile(name, rows.shape[2])
+            nc.scalar.copy(
+                grouped[:].rearrange("p (c i j) -> p c j i", i=4, j=PACK),
+                rows[:].rearrange("p j (c i) -> p c j i", i=4),
+            )
+            return grouped
+
+        v_words = [held([P, S], U32, "v_words%d" % a) for a in range(2)]
+        v_plane = held([P, S], U8, "v_plane")
+        h1 = [held([P, PACK, S], F32, "h1_%d" % b) for b in range(2)]
+        w1_q = {}
+
+        def first_product(b, t0, cols):
+            width = cols.stop - cols.start
+            slots = HALF // width
+            acc = psum.tile([P, slots, width], F32, name="acc_h1", tag="acc_h1", bufs=4)
+            for s in range(slots):
+                chans = slice(P * (t0 + s), P * (t0 + s + 1))
+                for a in range(2):
+                    codes, plane = w1_q[a, b]
+                    nc.tensor.matmul_mx(
+                        out=acc[:, s, :], lhsT=codes[:, chans].bitcast(FP8X4), lhsT_scale=plane[:, chans],
+                        rhs=v_words[a][:, cols].bitcast(FP8X4), rhs_scale=v_plane[4 * a :, cols],
+                        start=(a == 0), stop=(a == 1),
+                    )
+            nc.scalar.copy(h1[b][:, t0 : t0 + slots, cols], acc[:])
+
+        def first_products(b, cols):
+            for t0 in range(0, PACK, HALF // (cols.stop - cols.start)):
+                first_product(b, t0, cols)
+
+        def tanh_of(b, cols, bent=None):
+            if bent is None:
+                bent = ring.tile([P, PACK, cols.stop - cols.start], F32, name="bent", tag="bent", bufs=2)
+            nc.scalar.activation(bent[:], h1[b][:, :, cols], ACT.Tanh)
+            return bent
+
+        def floor_and_gain(b, bent):
+            rows = ring.tile([P, PACK, bent.shape[2]], BF16, name="z_rows", tag="z_rows", bufs=3)
+            for t in range(PACK):
+                nc.vector.tensor_scalar(
+                    rows[:, t, :], bent[:, t, :], least_tanh[:, b, t : t + 1], gain1_sb[:, b, t : t + 1], ALU.max, ALU.mult
+                )
+            return rows
+
+        def pick(b):
+            picked = ring.tile([P, PACK, PAIRS], F32, name="picked", tag="picked", bufs=1)
+            for t in range(PACK):
+                nc.vector.tensor_copy(picked[:, t, :], h1[b][:, t, :].indirect(pos[:]))
+            return picked
+
+        def angle_of(b, picked):
+            angle = tenant("slot_a", [P, PACK, PAIRS], F32, "angle")
+            for t in range(PACK):
+                chans = slice(PASS * b + P * t, PASS * b + P * (t + 1))
+                acc = psum.tile([P, PAIRS], F32, name="acc_h2", tag="acc_h2", bufs=2)
+                nc.tensor.matmul_mx(
+                    out=acc[:], lhsT=w2_codes[:, chans].bitcast(FP8X4), lhsT_scale=w2_plane[:, chans],
+                    rhs=v2_words[:].bitcast(FP8X4), rhs_scale=v2_plane[:], start=True, stop=True,
+                )
+                nc.vector.scalar_tensor_tensor(
+                    angle[:, t, :], picked[:, t, :], least_sb[:, b, t : t + 1], acc[:], ALU.max, ALU.add
+                )
+            return angle[:].rearrange("p t j -> p (t j)")
+
+        def whole_turns(angle):
+            whole = tenant("slot_b", [P, PACK * PAIRS], I32, "whole")
+            nc.vector.tensor_scalar(whole[:], angle, 1.0 / TURN, None, ALU.mult)
+            return whole
+
+        def rest_of_turn(angle, whole, rest):
+            nc.vector.scalar_tensor_tensor(rest, angle, 1.0 / TURN, whole[:], ALU.mult, ALU.subtract)
+            return rest
+
+        def sine_rows(b, rest):
+            nc.scalar.activation(rest, rest, ACT.Sin, scale=TURN)
+            sine = rest.rearrange("p (t j) -> p t j", t=PACK)
+            rows = ring.tile([P, PACK, PAIRS], BF16, name="z_rows", tag="z_rows", bufs=3)
+            for t in range(PACK):
+                nc.scalar.activation(rows[:, t, :], sine[:, t, :], ACT.Copy, scale=gain2_sb[:, b, t : t + 1])
+            return rows
+
+        def y1_sums(q, z1_q):
+            width = z1_q[0][0].shape[1]
+            acc = psum.tile([P, width], F32, name="acc_y", tag="acc_y", bufs=2)
+            for b in range(2):
+                codes, plane = z1_q[b]
+                nc.tensor.matmul_mx(
+                    out=acc[:], lhsT=w3_w[:, b, 2 * P * q : 2 * P * (q + 1)].bitcast(FP4X4),
+                    lhsT_scale=w3_plane[:, b, P * q : P * (q + 1)],
+                    rhs=codes[:].bitcast(FP8X4), rhs_scale=plane[:], start=(b == 0), stop=(b == 1),
+                )
+            sums = ring.tile([P, width], F32, name="sums", tag="sums", bufs=4)
+            nc.scalar.copy(sums[:], acc[:])
+            return sums
+
+        def put_y1(cols, q, sums):
+            lst = idx3[:, cols.start // PER_COL : cols.stop // PER_COL]
+            nc.vector.tensor_tensor(pages[q][:].indirect(lst), sums[:], wg1_sb[:, cols], ALU.mult)
+
+        def y2_sums(q, z2_q):
+            acc = psum.tile([P, PAIRS], F32, name="acc_y", tag="acc_y", bufs=2)
+            for b in range(2):
+                codes, plane = z2_q[b]
+                nc.tensor.matmul_mx(
+                    out=acc[:], lhsT=w4_q[b][0][:, P * q : P * (q + 1)].bitcast(FP8X4),
+                    lhsT_scale=w4_q[b][1][:, P * q : P * (q + 1)],
+                    rhs=codes[:].bitcast(FP8X4), rhs_scale=plane[:], start=(b == 0), stop=(b == 1),
+                )
+            sums = ring.tile([P, PAIRS], F32, name="sums", tag="sums", bufs=4)
+            nc.vector.tensor_tensor(sums[:], acc[:], cover_sb[:, q, :], ALU.mult)
+            return sums
+
+        nc.vector.tensor_copy(v_words[0][:], tab_w[0][:].bitcast(U32).indirect(idx[:]))
+        nc.vector.tensor_copy(v_plane[:], tab_plane[:].indirect(idx[:]))
+        w1_q[0, 0] = quantise(round_w1(0, 0, 0, grouped_tile("w1g", PASS)), "w1_00")
+        nc.vector.tensor_copy(v_words[1][:], tab_w[1][:].bitcast(U32).indirect(idx[:]))
+        w1_q[1, 0] = quantise(round_w1(1, 0, 64, grouped_tile("w1g", PASS)), "w1_10")
+        least_tanh = held([P, 2, PACK], F32, "least_tanh")
+        nc.scalar.activation(least_tanh[:], least_sb[:], ACT.Tanh)
+        for t in range(PACK):
+            for half in range(2):
+                first_product(0, t, slice(HALF * half, HALF * (half + 1)))
+
+        v2_words = held([P, PAIRS], U32, "v2_words")
+        v2_plane = held([P, PAIRS], U8, "v2_plane")
+        nc.vector.tensor_copy(v2_plane[:], tab2_plane[:].indirect(idx2[:]))
+        nc.vector.tensor_copy(v2_words[:], tab2_w[:].bitcast(U32).indirect(idx2[:]))
+        w2_codes = held([P, H], U32, "w2_codes")
+        w2_plane = held([P, H], U8, "w2_plane")
+        nc.vector.tensor_copy(
+            w2_plane[:].rearrange("p (b t m) -> p b m t", b=2, t=PACK),
+            w2_plane_raw[:].rearrange("p (b m t) -> p b m t", b=2, t=PACK),
+        )
+        nc.vector.tensor_copy(
+            w2_codes[:].rearrange("p (b t m) -> p b m t", b=2, t=PACK),
+            w2_raw[:].bitcast(U32).rearrange("p (b m t) -> p b m t", b=2, t=PACK),
+        )
+        picked0 = pick(0)
+        w1_q[0, 1] = quantise(round_w1(0, 1, 0, grouped_tile("w1g", PASS)), "w1_01")
+        w1_q[1, 1] = quantise(round_w1(1, 1, 0, tenant("slot_b", [P, PACK * PASS], BF16, "w1g_last")), "w1_11")
+        angle0 = angle_of(0, picked0)
+        whole0 = whole_turns(angle0)
+
+        def z1_of(rows, name):
+            return [quantise(interleave(rows[b], "z1g"), name + str(b)) for b in range(2)]
+
+        runs = [slice(0, 256), slice(256, 512), slice(512, 1024)]
+        rows_a = [floor_and_gain(0, tanh_of(0, runs[0], tenant("slot_c", [P, PACK, 256], F32, "bent_first")))]
+        rest0 = rest_of_turn(angle0, whole0, tenant("slot_c", [P, PACK * PAIRS], F32, "rest")[:])
+        first_products(1, runs[0])
+        rows_a.append(floor_and_gain(1, tanh_of(1, runs[0])))
+        first_products(1, runs[1])
+        z1_a = z1_of(rows_a, "z1_a")
+        rows_b = [floor_and_gain(b, tanh_of(b, runs[1])) for b in range(2)]
+        for q in range(4):
+            put_y1(runs[0], q, y1_sums(q, z1_a))
+        first_products(1, runs[2])
+        z1_b = z1_of(rows_b, "z1_b")
+        picked1 = pick(1)
+        angle1 = angle_of(1, picked1)
+        rows_c = [floor_and_gain(b, tanh_of(b, runs[2])) for b in range(2)]
+        rest1 = rest_of_turn(angle1, whole_turns(angle1), angle1)
+        rows20 = sine_rows(0, rest0)
+        z2_q = [quantise(interleave(rows20, "z2g"), "z2_0")]
+        for q in range(2):
+            put_y1(runs[1], q, y1_sums(q, z1_b))
+        z1_c = z1_of(rows_c, "z1_c")
+        for q in range(2, 4):
+            put_y1(runs[1], q, y1_sums(q, z1_b))
+        w4_q = [quantise(interleave(w4_raw[0], "w4g"), "w4_0")]
+        for q in range(2):
+            put_y1(runs[2], q, y1_sums(q, z1_c))
+        w4_q.append(quantise(interleave(w4_raw[1], "w4g"), "w4_1"))
+        rows21 = sine_rows(1, rest1)
+        put_y1(runs[2], 2, y1_sums(2, z1_c))
+        z2_q.append(quantise(interleave(rows21, "z2g"), "z2_1"))
+        put_y1(runs[2], 3, y1_sums(3, z1_c))
+        for q in range(4):
+            sums = y2_sums(q, z2_q)
+            nc.vector.tensor_tensor(pages[q][:].indirect(idx4[:]), sums[:], wg2_sb[:], ALU.mult)
+            nc.sync.dma_start(out[P * q : P * (q + 1), :], pages[q][:])

@@ -71,14 +71,18 @@ def tile_list_cyber_exposure_features_kernel(
         nc.vector.memset(w3_plane[:].rearrange("p a n -> p (a n)").bitcast(I32), 0)
 
         idx = load_list(offs, "idx")
-        tab_w = [load_words(tab_words[0], "tab_w0", "slot_a")]
         for q in range(4):
             nc.sync.dma_start(tab_plane[32 * q : 32 * q + 8, :].bitcast(I32), tab_scales[:, 4 * q : 4 * q + 4, :].bitcast(I32))
+        tab_w = [load_words(tab_words[0], "tab_w0", "slot_a")]
         least_sb = load_vector(nc.sync, least, "least_sb")
         w1_raw = {}
         w1_raw[0, 0] = load_rows(w1[0:PASS, 0:PASS], "w1_raw00")
-        tab_w.append(load_words(tab_words[1], "tab_w1", "slot_b"))
         idx2 = load_list(offs2, "idx2")
+        for q in range(4):
+            nc.sync.dma_start(tab2_plane[32 * q : 32 * q + 4, :].bitcast(I32), tab2_scales[0, 4 * q : 4 * q + 4, :].bitcast(I32))
+        tab_w.append(load_words(tab_words[1], "tab_w1", "slot_b"))
+        for q in range(4):
+            nc.sync.dma_start(w2_plane_raw[32 * q : 32 * q + 4, :].bitcast(I32), w2_scales[0, 4 * q : 4 * q + 4, :].bitcast(I32))
         w1_raw[1, 0] = load_rows(w1[PASS:, 0:PASS], "w1_raw10")
         pos = load_list(pos1, "pos")
         tab2_w = load_words(tab2_words[0], "tab2_w", "slot_c")
@@ -103,10 +107,6 @@ def tile_list_cyber_exposure_features_kernel(
         wg2_sb = held([P, PAIRS], F32, "wg2_sb")
         nc.sync.dma_start(wg2_sb[:], wg2)
 
-        for q in range(4):
-            nc.gpsimd.dma_start(tab2_plane[32 * q : 32 * q + 4, :].bitcast(I32), tab2_scales[0, 4 * q : 4 * q + 4, :].bitcast(I32))
-        for q in range(4):
-            nc.gpsimd.dma_start(w2_plane_raw[32 * q : 32 * q + 4, :].bitcast(I32), w2_scales[0, 4 * q : 4 * q + 4, :].bitcast(I32))
         gain1_sb = load_vector(nc.gpsimd, gain1, "gain1_sb")
         for q in range(4):
             nc.gpsimd.dma_start(
@@ -144,7 +144,7 @@ def tile_list_cyber_exposure_features_kernel(
 
         v_words = [held([P, S], U32, "v_words%d" % a) for a in range(2)]
         v_plane = held([P, S], U8, "v_plane")
-        h1 = [held([P, PACK, S], F32, "h1_%d" % b) for b in range(2)]
+        h1 = [tenant("h1_%d" % b, [P, PACK, S], F32, "h1_%d" % b) for b in range(2)]
         w1_q = {}
 
         def first_product(b, t0, cols):
@@ -210,8 +210,8 @@ def tile_list_cyber_exposure_features_kernel(
             return rest
 
         def sine_rows(b, rest):
-            nc.scalar.activation(rest, rest, ACT.Sin, scale=TURN)
-            sine = rest.rearrange("p (t j) -> p t j", t=PACK)
+            sine = tenant("h1_0", [P, PACK, PAIRS], F32, "sine")
+            nc.scalar.activation(sine[:].rearrange("p t j -> p (t j)"), rest, ACT.Sin, scale=TURN)
             rows = ring.tile([P, PACK, PAIRS], BF16, name="z_rows", tag="z_rows", bufs=3)
             for t in range(PACK):
                 nc.scalar.activation(rows[:, t, :], sine[:, t, :], ACT.Copy, scale=gain2_sb[:, b, t : t + 1])
@@ -248,16 +248,17 @@ def tile_list_cyber_exposure_features_kernel(
             nc.vector.tensor_tensor(sums[:], acc[:], cover_sb[:, q, :], ALU.mult)
             return sums
 
-        nc.vector.tensor_copy(v_words[0][:], tab_w[0][:].bitcast(U32).indirect(idx[:]))
         nc.vector.tensor_copy(v_plane[:], tab_plane[:].indirect(idx[:]))
+        nc.vector.tensor_copy(v_words[0][:], tab_w[0][:].bitcast(U32).indirect(idx[:]))
         w1_q[0, 0] = quantise(round_w1(0, 0, 0, grouped_tile("w1g", PASS)), "w1_00")
         nc.vector.tensor_copy(v_words[1][:], tab_w[1][:].bitcast(U32).indirect(idx[:]))
         w1_q[1, 0] = quantise(round_w1(1, 0, 64, grouped_tile("w1g", PASS)), "w1_10")
         least_tanh = held([P, 2, PACK], F32, "least_tanh")
         nc.scalar.activation(least_tanh[:], least_sb[:], ACT.Tanh)
-        for t in range(PACK):
-            for half in range(2):
-                first_product(0, t, slice(HALF * half, HALF * (half + 1)))
+        halves = [slice(0, HALF), slice(HALF, S)]
+        for t in range(2):
+            for cols in halves:
+                first_product(0, t, cols)
 
         v2_words = held([P, PAIRS], U32, "v2_words")
         v2_plane = held([P, PAIRS], U8, "v2_plane")
@@ -266,16 +267,19 @@ def tile_list_cyber_exposure_features_kernel(
         w2_codes = held([P, H], U32, "w2_codes")
         w2_plane = held([P, H], U8, "w2_plane")
         nc.vector.tensor_copy(
-            w2_plane[:].rearrange("p (b t m) -> p b m t", b=2, t=PACK),
-            w2_plane_raw[:].rearrange("p (b m t) -> p b m t", b=2, t=PACK),
+            w2_plane[:].rearrange("p (b t m) -> p b t m", b=2, t=PACK),
+            w2_plane_raw[:].rearrange("p (b m t) -> p b t m", b=2, t=PACK),
         )
         nc.vector.tensor_copy(
             w2_codes[:].rearrange("p (b t m) -> p b m t", b=2, t=PACK),
             w2_raw[:].bitcast(U32).rearrange("p (b m t) -> p b m t", b=2, t=PACK),
         )
-        picked0 = pick(0)
         w1_q[0, 1] = quantise(round_w1(0, 1, 0, grouped_tile("w1g", PASS)), "w1_01")
-        w1_q[1, 1] = quantise(round_w1(1, 1, 0, tenant("slot_b", [P, PACK * PASS], BF16, "w1g_last")), "w1_11")
+        w1_q[1, 1] = quantise(round_w1(1, 1, 32, grouped_tile("w1g", PASS)), "w1_11")
+        for t in range(2, PACK):
+            for cols in halves:
+                first_product(0, t, cols)
+        picked0 = pick(0)
         angle0 = angle_of(0, picked0)
         whole0 = whole_turns(angle0)
 
@@ -283,12 +287,12 @@ def tile_list_cyber_exposure_features_kernel(
             return [quantise(interleave(rows[b], "z1g"), name + str(b)) for b in range(2)]
 
         runs = [slice(0, 256), slice(256, 512), slice(512, 1024)]
-        rows_a = [floor_and_gain(0, tanh_of(0, runs[0], tenant("slot_c", [P, PACK, 256], F32, "bent_first")))]
-        rest0 = rest_of_turn(angle0, whole0, tenant("slot_c", [P, PACK * PAIRS], F32, "rest")[:])
         first_products(1, runs[0])
-        rows_a.append(floor_and_gain(1, tanh_of(1, runs[0])))
-        first_products(1, runs[1])
+        rows_a = [floor_and_gain(0, tanh_of(0, runs[0]))]
+        rows_a.append(floor_and_gain(1, tanh_of(1, runs[0], tenant("slot_c", [P, PACK, 256], F32, "bent_first"))))
+        rest0 = rest_of_turn(angle0, whole0, tenant("slot_c", [P, PACK * PAIRS], F32, "rest")[:])
         z1_a = z1_of(rows_a, "z1_a")
+        first_products(1, runs[1])
         rows_b = [floor_and_gain(b, tanh_of(b, runs[1])) for b in range(2)]
         for q in range(4):
             put_y1(runs[0], q, y1_sums(q, z1_a))
@@ -308,10 +312,9 @@ def tile_list_cyber_exposure_features_kernel(
         w4_q = [quantise(interleave(w4_raw[0], "w4g"), "w4_0")]
         for q in range(2):
             put_y1(runs[2], q, y1_sums(q, z1_c))
-        w4_q.append(quantise(interleave(w4_raw[1], "w4g"), "w4_1"))
-        rows21 = sine_rows(1, rest1)
+        z2_q.append(quantise(interleave(sine_rows(1, rest1), "z2g"), "z2_1"))
         put_y1(runs[2], 2, y1_sums(2, z1_c))
-        z2_q.append(quantise(interleave(rows21, "z2g"), "z2_1"))
+        w4_q.append(quantise(interleave(w4_raw[1], "w4g"), "w4_1"))
         put_y1(runs[2], 3, y1_sums(3, z1_c))
         for q in range(4):
             sums = y2_sums(q, z2_q)

import math
from contextlib import ExitStack

import concourse.mybir as mybir

F32 = mybir.dt.float32
BF16 = mybir.dt.bfloat16
I32 = mybir.dt.int32
U32 = mybir.dt.uint32
U16 = mybir.dt.uint16
U8 = mybir.dt.uint8
FP8X4 = mybir.dt.float8_e4m3fn_x4
FP4X4 = mybir.dt.float4_e2m1fn_x4
ALU = mybir.AluOpType
ACT = mybir.ActivationFunctionType

K, K2, H, N, T, S, PAIRS, T2 = 1024, 512, 1024, 512, 2048, 1024, 512, 2048
FLOPS = 2 * (K * H * S + K2 * H * PAIRS + H * N * S + H * N * PAIRS)

P = 128
PACK = 4
PASS = P * PACK
HALF = 512
PER_COL = 16
TURN = 2.0 * math.pi


def tile_list_cyber_exposure_features_kernel(
    tc, tab_words, tab_scales, offs, tab2_words, tab2_scales, offs2, pos1, w1, least, w2_words, w2_scales,
    gain1, gain2, w3_words, w3_scales, w4, cover, page1, wg1, wg2, offs3, offs4, out,
):
    nc = tc.nc
    with ExitStack() as ctx:
        keep = ctx.enter_context(tc.tile_pool(name="keep", bufs=1))
        ring = ctx.enter_context(tc.tile_pool(name="ring", bufs=2))
        psum = ctx.enter_context(tc.psum_pool(name="psum", bufs=1))

        def held(shape, dtype, name):
            return keep.tile(shape, dtype, name=name, align_bytes=64)

        def load_list(src, name):
            lst = keep.tile([P, src.shape[1]], U16, name=name)
            nc.sync.dma_start(lst[:], src)
            return lst

        def tenant(slot, shape, dtype, name):
            return keep.tile(shape, dtype, name=name, tag=slot, align_bytes=64)

        def load_words(src, name, slot):
            words = tenant(slot, [P, T], I32, name)
            nc.sync.dma_start(words[:], src.rearrange("p n i -> p (n i)").bitcast(I32))
            return words

        def load_rows(src, name):
            raw = ring.tile([P, PACK, HALF], F32, name=name, tag="raw", bufs=3)
            nc.sync.dma_start(raw[:], src.rearrange("(p j) c -> p j c", j=PACK))
            return raw

        def load_vector(queue, src, name):
            vec = held([P, 2, PACK], F32, name)
            queue.dma_start(vec[:], src.rearrange("(b p t) -> p b t", p=P, t=PACK))
            return vec

        tab_plane = held([P, T], U8, "tab_plane")
        tab2_plane = held([P, T], U8, "tab2_plane")
        w2_plane_raw = held([P, H], U8, "w2_plane_raw")
        w3_plane = held([P, 2, N], U8, "w3_plane")
        nc.gpsimd.memset(tab_plane[:].bitcast(I32), 0)
        nc.vector.memset(tab2_plane[:].bitcast(I32), 0)
        nc.vector.memset(w2_plane_raw[:].bitcast(I32), 0)
        nc.vector.memset(w3_plane[:].rearrange("p a n -> p (a n)").bitcast(I32), 0)

        idx = load_list(offs, "idx")
        for q in range(4):
            nc.sync.dma_start(tab_plane[32 * q : 32 * q + 8, :].bitcast(I32), tab_scales[:, 4 * q : 4 * q + 4, :].bitcast(I32))
        tab_w = [load_words(tab_words[0], "tab_w0", "slot_a")]
        least_sb = load_vector(nc.sync, least, "least_sb")
        w1_raw = {}
        w1_raw[0, 0] = load_rows(w1[0:PASS, 0:PASS], "w1_raw00")
        idx2 = load_list(offs2, "idx2")
        for q in range(4):
            nc.sync.dma_start(tab2_plane[32 * q : 32 * q + 4, :].bitcast(I32), tab2_scales[0, 4 * q : 4 * q + 4, :].bitcast(I32))
        tab_w.append(load_words(tab_words[1], "tab_w1", "slot_b"))
        for q in range(4):
            nc.sync.dma_start(w2_plane_raw[32 * q : 32 * q + 4, :].bitcast(I32), w2_scales[0, 4 * q : 4 * q + 4, :].bitcast(I32))
        w1_raw[1, 0] = load_rows(w1[PASS:, 0:PASS], "w1_raw10")
        pos = load_list(pos1, "pos")
        tab2_w = load_words(tab2_words[0], "tab2_w", "slot_c")
        w2_raw = held([P, H], I32, "w2_raw")
        nc.sync.dma_start(w2_raw[:], w2_words[0].rearrange("p n i -> p (n i)").bitcast(I32))
        w1_raw[0, 1] = load_rows(w1[0:PASS, PASS:], "w1_raw01")
        w1_raw[1, 1] = load_rows(w1[PASS:, PASS:], "w1_raw11")
        w3_w = held([P, 2, 2 * N], U8, "w3_w")
        nc.sync.dma_start(w3_w[:].bitcast(I32), w3_words.rearrange("a p n -> p a n").bitcast(I32))
        idx3 = load_list(offs3, "idx3")
        idx4 = load_list(offs4, "idx4")
        wg1_sb = held([P, S], F32, "wg1_sb")
        nc.sync.dma_start(wg1_sb[:], wg1)
        pages = []
        for q in range(N // P):
            page = held([P, T2], F32, "page%d" % q)
            nc.sync.dma_start(page[:], page1[P * q : P * (q + 1), :])
            pages.append(page)
        w4_raw = [load_rows(w4[PASS * b : PASS * (b + 1), :], "w4_raw%d" % b) for b in range(2)]
        cover_sb = ring.tile([P, N // P, PAIRS], F32, name="cover_sb", tag="raw", bufs=3)
        nc.sync.dma_start(cover_sb[:], cover.rearrange("(q p) j -> p q j", p=P))
        wg2_sb = held([P, PAIRS], F32, "wg2_sb")
        nc.sync.dma_start(wg2_sb[:], wg2)

        gain1_sb = load_vector(nc.gpsimd, gain1, "gain1_sb")
        for q in range(4):
            nc.gpsimd.dma_start(
                w3_plane[32 * q : 32 * q + 4, :, :].bitcast(I32),
                w3_scales[:, 4 * q : 4 * q + 4, :].rearrange("a r n -> r a n").bitcast(I32),
            )
        gain2_sb = load_vector(nc.gpsimd, gain2, "gain2_sb")

        def quantise(grouped, name):
            width = grouped.shape[1] // PACK
            codes = held([P, width], U32, name + "_codes")
            plane = held([P, width], U8, name + "_plane")
            nc.vector.quantize_mx(out=codes[:].bitcast(FP8X4), scales=plane[:], in_=grouped[:])
            return codes, plane

        def grouped_tile(name, width):
            return ring.tile([P, PACK * width], BF16, name=name, tag="grouped", bufs=3, align_bytes=64)

        def round_w1(a, b, vector_share, grouped):
            dst = grouped[:].rearrange("p (t m j) -> p m j t", t=PACK, j=PACK)
            src = w1_raw[a, b][:].rearrange("p j (m t) -> p m j t", t=PACK)
            cut = P - vector_share
            nc.scalar.copy(dst[:, :cut], src[:, :cut])
            if vector_share:
                nc.vector.tensor_copy(dst[:, cut:], src[:, cut:])
            return grouped

        def interleave(rows, name):
            grouped = grouped_tile(name, rows.shape[2])
            nc.scalar.copy(
                grouped[:].rearrange("p (c i j) -> p c j i", i=4, j=PACK),
                rows[:].rearrange("p j (c i) -> p c j i", i=4),
            )
            return grouped

        v_words = [held([P, S], U32, "v_words%d" % a) for a in range(2)]
        v_plane = held([P, S], U8, "v_plane")
        h1 = [tenant("h1_%d" % b, [P, PACK, S], F32, "h1_%d" % b) for b in range(2)]
        w1_q = {}

        def first_product(b, t0, cols):
            width = cols.stop - cols.start
            slots = HALF // width
            acc = psum.tile([P, slots, width], F32, name="acc_h1", tag="acc_h1", bufs=4)
            for s in range(slots):
                chans = slice(P * (t0 + s), P * (t0 + s + 1))
                for a in range(2):
                    codes, plane = w1_q[a, b]
                    nc.tensor.matmul_mx(
                        out=acc[:, s, :], lhsT=codes[:, chans].bitcast(FP8X4), lhsT_scale=plane[:, chans],
                        rhs=v_words[a][:, cols].bitcast(FP8X4), rhs_scale=v_plane[4 * a :, cols],
                        start=(a == 0), stop=(a == 1),
                    )
            nc.scalar.copy(h1[b][:, t0 : t0 + slots, cols], acc[:])

        def first_products(b, cols):
            for t0 in range(0, PACK, HALF // (cols.stop - cols.start)):
                first_product(b, t0, cols)

        def tanh_of(b, cols, bent=None):
            if bent is None:
                bent = ring.tile([P, PACK, cols.stop - cols.start], F32, name="bent", tag="bent", bufs=2)
            nc.scalar.activation(bent[:], h1[b][:, :, cols], ACT.Tanh)
            return bent

        def floor_and_gain(b, bent):
            rows = ring.tile([P, PACK, bent.shape[2]], BF16, name="z_rows", tag="z_rows", bufs=3)
            for t in range(PACK):
                nc.vector.tensor_scalar(
                    rows[:, t, :], bent[:, t, :], least_tanh[:, b, t : t + 1], gain1_sb[:, b, t : t + 1], ALU.max, ALU.mult
                )
            return rows

        def pick(b):
            picked = ring.tile([P, PACK, PAIRS], F32, name="picked", tag="picked", bufs=1)
            for t in range(PACK):
                nc.vector.tensor_copy(picked[:, t, :], h1[b][:, t, :].indirect(pos[:]))
            return picked

        def angle_of(b, picked):
            angle = tenant("slot_a", [P, PACK, PAIRS], F32, "angle")
            for t in range(PACK):
                chans = slice(PASS * b + P * t, PASS * b + P * (t + 1))
                acc = psum.tile([P, PAIRS], F32, name="acc_h2", tag="acc_h2", bufs=2)
                nc.tensor.matmul_mx(
                    out=acc[:], lhsT=w2_codes[:, chans].bitcast(FP8X4), lhsT_scale=w2_plane[:, chans],
                    rhs=v2_words[:].bitcast(FP8X4), rhs_scale=v2_plane[:], start=True, stop=True,
                )
                nc.vector.scalar_tensor_tensor(
                    angle[:, t, :], picked[:, t, :], least_sb[:, b, t : t + 1], acc[:], ALU.max, ALU.add
                )
            return angle[:].rearrange("p t j -> p (t j)")

        def whole_turns(angle):
            whole = tenant("slot_b", [P, PACK * PAIRS], I32, "whole")
            nc.vector.tensor_scalar(whole[:], angle, 1.0 / TURN, None, ALU.mult)
            return whole

        def rest_of_turn(angle, whole, rest):
            nc.vector.scalar_tensor_tensor(rest, angle, 1.0 / TURN, whole[:], ALU.mult, ALU.subtract)
            return rest

        def sine_rows(b, rest):
            sine = tenant("h1_0", [P, PACK, PAIRS], F32, "sine")
            nc.scalar.activation(sine[:].rearrange("p t j -> p (t j)"), rest, ACT.Sin, scale=TURN)
            rows = ring.tile([P, PACK, PAIRS], BF16, name="z_rows", tag="z_rows", bufs=3)
            for t in range(PACK):
                nc.scalar.activation(rows[:, t, :], sine[:, t, :], ACT.Copy, scale=gain2_sb[:, b, t : t + 1])
            return rows

        def y1_sums(q, z1_q):
            width = z1_q[0][0].shape[1]
            acc = psum.tile([P, width], F32, name="acc_y", tag="acc_y", bufs=2)
            for b in range(2):
                codes, plane = z1_q[b]
                nc.tensor.matmul_mx(
                    out=acc[:], lhsT=w3_w[:, b, 2 * P * q : 2 * P * (q + 1)].bitcast(FP4X4),
                    lhsT_scale=w3_plane[:, b, P * q : P * (q + 1)],
                    rhs=codes[:].bitcast(FP8X4), rhs_scale=plane[:], start=(b == 0), stop=(b == 1),
                )
            sums = ring.tile([P, width], F32, name="sums", tag="sums", bufs=4)
            nc.scalar.copy(sums[:], acc[:])
            return sums

        def put_y1(cols, q, sums):
            lst = idx3[:, cols.start // PER_COL : cols.stop // PER_COL]
            nc.vector.tensor_tensor(pages[q][:].indirect(lst), sums[:], wg1_sb[:, cols], ALU.mult)

        def y2_sums(q, z2_q):
            acc = psum.tile([P, PAIRS], F32, name="acc_y", tag="acc_y", bufs=2)
            for b in range(2):
                codes, plane = z2_q[b]
                nc.tensor.matmul_mx(
                    out=acc[:], lhsT=w4_q[b][0][:, P * q : P * (q + 1)].bitcast(FP8X4),
                    lhsT_scale=w4_q[b][1][:, P * q : P * (q + 1)],
                    rhs=codes[:].bitcast(FP8X4), rhs_scale=plane[:], start=(b == 0), stop=(b == 1),
                )
            sums = ring.tile([P, PAIRS], F32, name="sums", tag="sums", bufs=4)
            nc.vector.tensor_tensor(sums[:], acc[:], cover_sb[:, q, :], ALU.mult)
            return sums

        nc.vector.tensor_copy(v_plane[:], tab_plane[:].indirect(idx[:]))
        nc.vector.tensor_copy(v_words[0][:], tab_w[0][:].bitcast(U32).indirect(idx[:]))
        w1_q[0, 0] = quantise(round_w1(0, 0, 0, grouped_tile("w1g", PASS)), "w1_00")
        nc.vector.tensor_copy(v_words[1][:], tab_w[1][:].bitcast(U32).indirect(idx[:]))
        w1_q[1, 0] = quantise(round_w1(1, 0, 64, grouped_tile("w1g", PASS)), "w1_10")
        least_tanh = held([P, 2, PACK], F32, "least_tanh")
        nc.scalar.activation(least_tanh[:], least_sb[:], ACT.Tanh)
        halves = [slice(0, HALF), slice(HALF, S)]
        for t in range(2):
            for cols in halves:
                first_product(0, t, cols)

        v2_words = held([P, PAIRS], U32, "v2_words")
        v2_plane = held([P, PAIRS], U8, "v2_plane")
        nc.vector.tensor_copy(v2_plane[:], tab2_plane[:].indirect(idx2[:]))
        nc.vector.tensor_copy(v2_words[:], tab2_w[:].bitcast(U32).indirect(idx2[:]))
        w2_codes = held([P, H], U32, "w2_codes")
        w2_plane = held([P, H], U8, "w2_plane")
        nc.vector.tensor_copy(
            w2_plane[:].rearrange("p (b t m) -> p b t m", b=2, t=PACK),
            w2_plane_raw[:].rearrange("p (b m t) -> p b t m", b=2, t=PACK),
        )
        nc.vector.tensor_copy(
            w2_codes[:].rearrange("p (b t m) -> p b m t", b=2, t=PACK),
            w2_raw[:].bitcast(U32).rearrange("p (b m t) -> p b m t", b=2, t=PACK),
        )
        w1_q[0, 1] = quantise(round_w1(0, 1, 0, grouped_tile("w1g", PASS)), "w1_01")
        w1_q[1, 1] = quantise(round_w1(1, 1, 32, grouped_tile("w1g", PASS)), "w1_11")
        for t in range(2, PACK):
            for cols in halves:
                first_product(0, t, cols)
        picked0 = pick(0)
        angle0 = angle_of(0, picked0)
        whole0 = whole_turns(angle0)

        def z1_of(rows, name):
            return [quantise(interleave(rows[b], "z1g"), name + str(b)) for b in range(2)]

        runs = [slice(0, 256), slice(256, 512), slice(512, 1024)]
        first_products(1, runs[0])
        rows_a = [floor_and_gain(0, tanh_of(0, runs[0]))]
        rows_a.append(floor_and_gain(1, tanh_of(1, runs[0], tenant("slot_c", [P, PACK, 256], F32, "bent_first"))))
        rest0 = rest_of_turn(angle0, whole0, tenant("slot_c", [P, PACK * PAIRS], F32, "rest")[:])
        z1_a = z1_of(rows_a, "z1_a")
        first_products(1, runs[1])
        rows_b = [floor_and_gain(b, tanh_of(b, runs[1])) for b in range(2)]
        for q in range(4):
            put_y1(runs[0], q, y1_sums(q, z1_a))
        first_products(1, runs[2])
        z1_b = z1_of(rows_b, "z1_b")
        picked1 = pick(1)
        angle1 = angle_of(1, picked1)
        rows_c = [floor_and_gain(b, tanh_of(b, runs[2])) for b in range(2)]
        rest1 = rest_of_turn(angle1, whole_turns(angle1), angle1)
        rows20 = sine_rows(0, rest0)
        z2_q = [quantise(interleave(rows20, "z2g"), "z2_0")]
        for q in range(2):
            put_y1(runs[1], q, y1_sums(q, z1_b))
        z1_c = z1_of(rows_c, "z1_c")
        for q in range(2, 4):
            put_y1(runs[1], q, y1_sums(q, z1_b))
        w4_q = [quantise(interleave(w4_raw[0], "w4g"), "w4_0")]
        for q in range(2):
            put_y1(runs[2], q, y1_sums(q, z1_c))
        z2_q.append(quantise(interleave(sine_rows(1, rest1), "z2g"), "z2_1"))
        put_y1(runs[2], 2, y1_sums(2, z1_c))
        w4_q.append(quantise(interleave(w4_raw[1], "w4g"), "w4_1"))
        put_y1(runs[2], 3, y1_sums(3, z1_c))
        for q in range(4):
            sums = y2_sums(q, z2_q)
            nc.vector.tensor_tensor(pages[q][:].indirect(idx4[:]), sums[:], wg2_sb[:], ALU.mult)
            nc.sync.dma_start(out[P * q : P * (q + 1), :], pages[q][:])
